import numpy as np, ml_dtypes
CORES = [113,118,241,246]
N = 4
TK = 64
def gelu(z): return 0.5 * z * (1.0 + np.tanh(0.7978845608028654 * (z + 0.044715 * z ** 3)))
def setup_inputs(rng):
    return {"x": rng.standard_normal((N, 128, TK), dtype=np.float32).astype(ml_dtypes.bfloat16), "w1": (rng.standard_normal((N, 128, 128), dtype=np.float32) / 8).astype(ml_dtypes.bfloat16), "w2": (rng.standard_normal((N, 128, 128), dtype=np.float32) / 8).astype(ml_dtypes.bfloat16)}
def setup_inputs_big(rng):
    d = setup_inputs(rng)
    for k in ("x",): d[k] = (d[k].astype(np.float32) * 1024.0).astype(d[k].dtype)
    return d
def setup_inputs_small(rng):
    d = setup_inputs(rng)
    for k in ("x",): d[k] = (d[k].astype(np.float32) * (1 / 1024.0)).astype(d[k].dtype)
    return d
def setup_inputs_apart(rng):
    d = setup_inputs(rng)
    f = (10.0 ** rng.permutation(np.linspace(-1.5, 1.5, N))).astype(np.float32).reshape(N, 1, 1)
    for k in ("x",): d[k] = (d[k].astype(np.float32) * f).astype(d[k].dtype)
    return d
def reference(x, w1, w2):
    X, W1, W2 = x.astype(np.float64), w1.astype(np.float64), w2.astype(np.float64)
    y = np.zeros((N, 128, TK))
    for r in range(N):
        for j in range(N):
            y[r] += W2[j].T @ (gelu(W1[j].T @ X[r]))
    return {"y": y.astype(ml_dtypes.bfloat16)}

from concourse.bass import DstId, RemoteDMATransfer
from concourse.mybir import ActivationFunctionType

N = 4
TK = 64
D = 128
SLOT = 2 * D

SCRATCH = {
    "wall": ("sbuf", [128, N * SLOT], "bfloat16"),
    "xs": ("sbuf", [128, TK], "bfloat16"),
    "hs": ("sbuf", [128, N * TK], "bfloat16"),
    "ys": ("sbuf", [128, TK], "bfloat16"),
    "py": ("psum", [128, 512], "float32"),
}
for _j in range(N):
    SCRATCH["ph%d" % _j] = ("psum", [128, 512], "float32")

SEMAPHORES = (["ldw", "ldx", "sent", "m2", "cp", "st"]
              + ["arr%d" % j for j in range(N)] + ["m1_%d" % j for j in range(N)] + ["ge%d" % j for j in range(N)])


def _bits(mask):
    return [1 << b for b in range(mask.bit_length()) if (mask >> b) & 1]


def _join(bits):
    m = 0
    for b in bits:
        m |= b
    return m


def _pow2_floor(n):
    p = 1
    while p * 2 <= n:
        p *= 2
    return p


def _same_chip(topo, a, b):
    return topo.host(a) == topo.host(b) and topo.chip(a) == topo.chip(b)


def _plan(topo, cores, src):
    far = [d for d in cores if d != src and not _same_chip(topo, src, d)]
    near = [d for d in cores if d != src and _same_chip(topo, src, d)]
    used = 0
    far_plan, near_plan = [], []
    if far:
        common = topo.mask(src, far[0])
        for d in far:
            common &= topo.mask(src, d)
        eng = _bits(common)
        share = _pow2_floor(len(eng) // len(far))
        for i, d in enumerate(far):
            m = _join(eng[i * share:(i + 1) * share])
            far_plan.append((d, m))
            used |= m
    if near:
        common = topo.mask(src, near[0])
        for d in near:
            common &= topo.mask(src, d)
        eng = _bits(common & ~used)
        share = _pow2_floor(len(eng) // len(near))
        for i, d in enumerate(near):
            near_plan.append((d, _join(eng[i * share:(i + 1) * share])))
    return far_plan, near_plan


def rank_program(g, core, T, topo):
    rank = T.rank_of(core)
    if rank is None:
        return
    cores = list(T.cores)
    sem = T.sem

    def slot(j):
        return T.wall[:, j * SLOT:(j + 1) * SLOT]

    def w1(j):
        return T.wall[:, j * SLOT:j * SLOT + D]

    def w2(j):
        return T.wall[:, j * SLOT + D:(j + 1) * SLOT]

    def h(j):
        return T.hs[:, j * TK:(j + 1) * TK]

    g.sync.dma_start(w1(rank), T.w1[:]).then_inc(sem.ldw, 16)
    g.scalar.dma_start(w2(rank), T.w2[:]).then_inc(sem.ldw, 16)
    g.sync.dma_start(T.xs[:], T.x[:]).then_inc(sem.ldx, 16)

    far_plan, near_plan = _plan(topo, cores, core)
    g.wait_ge(sem.ldw, 32)
    sent = 0
    transfers = []
    for d, m in far_plan:
        rid, pid = topo.addr(d, core)
        transfers.append(RemoteDMATransfer(dst_ids=[DstId(rid=rid, pnc=pid)], dma_engine_mask=m,
                                           remote_sem=sem["arr%d" % rank], src=slot(rank), dst=slot(rank)))
        sent += len(_bits(m))
    g.remote_dma_fused(transfers, local_sem=sem.sent)
    for d, m in near_plan:
        rid, pid = topo.addr(d, core)
        g.remote_dma(slot(rank), slot(rank), sem["arr%d" % rank], sem.sent, pid, rid, m)
        sent += len(_bits(m))

    def arrival(j):
        fp, np_ = _plan(topo, cores, cores[j])
        for d, m in fp + np_:
            if d == core:
                return len(_bits(m))
        return 0

    others = [j for j in range(len(cores)) if j != rank]
    others.sort(key=lambda j: (not _same_chip(topo, core, cores[j]), topo.die(cores[j]) != topo.die(core)))
    order = [rank] + others

    def mm1(j):
        g.tensor.matmul(T["ph%d" % j][:, 0:TK], w1(j), T.xs[:], True, True).then_inc(sem["m1_%d" % j], 1)

    def mm2(j):
        g.tensor.wait_ge(sem["ge%d" % j], 1)
        g.tensor.matmul(T.py[:, 0:TK], w2(j), h(j), j == order[0], j == order[-1]).then_inc(sem.m2, 1)

    g.tensor.wait_ge(sem.ldw, 32)
    g.tensor.wait_ge(sem.ldx, 16)
    mm1(order[0])
    for k in range(1, len(order)):
        j = order[k]
        g.tensor.wait_ge(sem["arr%d" % j], arrival(j))
        mm1(j)
        mm2(order[k - 1])
    mm2(order[-1])

    for j in order:
        g.scalar.wait_ge(sem["m1_%d" % j], 1)
        g.scalar.activation(h(j), T["ph%d" % j][:, 0:TK], ActivationFunctionType.Gelu_apprx_tanh).then_inc(sem["ge%d" % j], 1)

    g.vector.wait_ge(sem.m2, len(order))
    g.vector.tensor_copy(T.ys[:], T.py[:, 0:TK]).then_inc(sem.cp, 1)
    g.sync.wait_ge(sem.cp, 1)
    g.sync.dma_start(T.y[:], T.ys[:]).then_inc(sem.st, 16)
    g.sync.wait_ge(sem.st, 16)

    g.wait_ge(sem.sent, sent)
